import numpy as np, ml_dtypes
CORES = [4,20,36,52,68,84,100,116,12,28,44,60,76,92,108,124]
N = 16
def setup_inputs(rng):
    return {"x": rng.standard_normal((N, 128, 512), dtype=np.float32).astype(ml_dtypes.bfloat16)}
def reference(x):
    s = x.max(axis=0)
    b = 512 // N
    return {"y": np.stack([s[:, r * b:(r + 1) * b] for r in range(N)])}

@@ -1,0 +1,67 @@
+from concourse.bass import DstId, RemoteDMATransfer
+
+A = 1
+NB = 8 // A
+
+SCRATCH = {
+    "xs": ("dram", [16, 128, 32], "bfloat16"),
+    "ca": ("dram", [8, 128, 32], "bfloat16"),
+    "cb": ("dram", [9, 128, 32], "bfloat16"),
+    "res": ("dram", [NB, 128, 32], "bfloat16"),
+}
+SEMAPHORES = ["la", "lb", "sent", "arra", "arrb", "arrr", "stored"]
+
+RANK_K, MATE_K, FOLD_K = 4, 6, 7
+
+
+def rank_program(g, core, T, topo):
+    ch = topo.chip(core)
+    k = core % 8
+    p = ch & 1
+    j = ch >> 1
+    sem = T.sem
+
+    def cid(pp, jj, kk):
+        return (2 * jj + pp) * 8 + kk
+
+    def dst(c):
+        a = topo.addr(c)
+        return DstId(rid=a[0], pnc=a[1])
+
+    if k == RANK_K:
+        q = 1 - p
+        queues = [g.sync, g.scalar]
+        n = 0
+        for h, s in ((q, sem.la), (p, sem.lb)):
+            for ga in range(A):
+                c0 = 256 * h + ga * 32 * NB
+                queues[n % 2].dma_start(T.xs[8 * h + ga * NB:8 * h + (ga + 1) * NB],
+                                        T.x[:, c0:c0 + 32 * NB]).then_inc(s, 16)
+                n += 1
+        for h, s, kk, buf, rs in ((q, sem.la, MATE_K, T.ca, sem.arra), (p, sem.lb, FOLD_K, T.cb, sem.arrb)):
+            g.wait_ge(s, 16 * A)
+            g.remote_dma_fused(
+                [RemoteDMATransfer(dst_ids=[dst(cid(p, jj, kk))], dma_engine_mask=1 << jj, remote_sem=rs,
+                                   src=T.xs[8 * h + jj], dst=buf[j]) for jj in range(8)],
+                local_sem=sem.sent)
+        kb = j % NB
+        g.sync.wait_ge(sem.arrr, 8 * NB)
+        g.sync.dma_start(T.y[:], T.res[:, kb::NB, :] if NB > 1 else T.res[0]).then_inc(sem.stored, 16)
+        g.wait_ge(sem.sent, 16)
+        g.sync.wait_ge(sem.stored, 16)
+    elif k == MATE_K:
+        g.wait_ge(sem.arra, 8)
+        g.remote_dma_fused(
+            [RemoteDMATransfer(dst_ids=[dst(cid(1 - p, j, FOLD_K))], dma_engine_mask=0xFF, remote_sem=sem.arrb,
+                               srcs=[T.ca[i] for i in range(8)], dsts=[T.cb[8]], alu_op=2)],
+            local_sem=sem.sent)
+        g.wait_ge(sem.sent, 8)
+    elif k == FOLD_K:
+        ga, jb = divmod(j, NB)
+        g.wait_ge(sem.arrb, 16)
+        g.remote_dma_fused(
+            [RemoteDMATransfer(dst_ids=[dst(cid(p, ga * NB + kb, RANK_K)) for kb in range(NB)], dma_engine_mask=0xFF,
+                               remote_sem=sem.arrr, srcs=[T.cb[i] for i in range(9)],
+                               dsts=[T.res[jb] for kb in range(NB)], alu_op=2)],
+            local_sem=sem.sent)
+        g.wait_ge(sem.sent, 8)

@@ -1,6 +1,6 @@
 from concourse.bass import DstId, RemoteDMATransfer
 
-A = 1
+A = 2
 NB = 8 // A
 
 SCRATCH = {

@@ -1,6 +1,6 @@
 from concourse.bass import DstId, RemoteDMATransfer
 
-A = 2
+A = 4
 NB = 8 // A
 
 SCRATCH = {

@@ -1,7 +1,9 @@
 from concourse.bass import DstId, RemoteDMATransfer
 
-A = 4
+A = 8
 NB = 8 // A
+W3_MASK = 0xFFFF if NB == 1 else 0xFF
+W3_ENG = 16 if NB == 1 else 8
 
 SCRATCH = {
     "xs": ("dram", [16, 128, 32], "bfloat16"),
@@ -45,7 +47,7 @@ def rank_program(g, core, T, topo):
                                    src=T.xs[8 * h + jj], dst=buf[j]) for jj in range(8)],
                 local_sem=sem.sent)
         kb = j % NB
-        g.sync.wait_ge(sem.arrr, 8 * NB)
+        g.sync.wait_ge(sem.arrr, W3_ENG * NB)
         g.sync.dma_start(T.y[:], T.res[:, kb::NB, :] if NB > 1 else T.res[0]).then_inc(sem.stored, 16)
         g.wait_ge(sem.sent, 16)
         g.sync.wait_ge(sem.stored, 16)
@@ -60,8 +62,8 @@ def rank_program(g, core, T, topo):
         ga, jb = divmod(j, NB)
         g.wait_ge(sem.arrb, 16)
         g.remote_dma_fused(
-            [RemoteDMATransfer(dst_ids=[dst(cid(p, ga * NB + kb, RANK_K)) for kb in range(NB)], dma_engine_mask=0xFF,
-                               remote_sem=sem.arrr, srcs=[T.cb[i] for i in range(9)],
+            [RemoteDMATransfer(dst_ids=[dst(cid(p, ga * NB + kb, RANK_K)) for kb in range(NB)],
+                               dma_engine_mask=W3_MASK, remote_sem=sem.arrr, srcs=[T.cb[i] for i in range(9)],
                                dsts=[T.res[jb] for kb in range(NB)], alu_op=2)],
             local_sem=sem.sent)
-        g.wait_ge(sem.sent, 8)
+        g.wait_ge(sem.sent, W3_ENG)

@@ -1,19 +1,15 @@
 from concourse.bass import DstId, RemoteDMATransfer
 
-A = 8
-NB = 8 // A
-W3_MASK = 0xFFFF if NB == 1 else 0xFF
-W3_ENG = 16 if NB == 1 else 8
-
 SCRATCH = {
     "xs": ("dram", [16, 128, 32], "bfloat16"),
-    "ca": ("dram", [8, 128, 32], "bfloat16"),
-    "cb": ("dram", [9, 128, 32], "bfloat16"),
-    "res": ("dram", [NB, 128, 32], "bfloat16"),
+    "ca": ("dram", [4, 128, 32], "bfloat16"),
+    "cb": ("dram", [10, 128, 32], "bfloat16"),
+    "res": ("dram", [128, 32], "bfloat16"),
 }
 SEMAPHORES = ["la", "lb", "sent", "arra", "arrb", "arrr", "stored"]
 
-RANK_K, MATE_K, FOLD_K = 4, 6, 7
+RANK_K, FOLD_K = 4, 5
+MATE_KS = (6, 7)
 
 
 def rank_program(g, core, T, topo):
@@ -33,37 +29,36 @@ def rank_program(g, core, T, topo):
     if k == RANK_K:
         q = 1 - p
         queues = [g.sync, g.scalar]
-        n = 0
         for h, s in ((q, sem.la), (p, sem.lb)):
-            for ga in range(A):
-                c0 = 256 * h + ga * 32 * NB
-                queues[n % 2].dma_start(T.xs[8 * h + ga * NB:8 * h + (ga + 1) * NB],
-                                        T.x[:, c0:c0 + 32 * NB]).then_inc(s, 16)
-                n += 1
-        for h, s, kk, buf, rs in ((q, sem.la, MATE_K, T.ca, sem.arra), (p, sem.lb, FOLD_K, T.cb, sem.arrb)):
-            g.wait_ge(s, 16 * A)
-            g.remote_dma_fused(
-                [RemoteDMATransfer(dst_ids=[dst(cid(p, jj, kk))], dma_engine_mask=1 << jj, remote_sem=rs,
-                                   src=T.xs[8 * h + jj], dst=buf[j]) for jj in range(8)],
-                local_sem=sem.sent)
-        kb = j % NB
-        g.sync.wait_ge(sem.arrr, W3_ENG * NB)
-        g.sync.dma_start(T.y[:], T.res[:, kb::NB, :] if NB > 1 else T.res[0]).then_inc(sem.stored, 16)
+            for jj in range(8):
+                c0 = 256 * h + 32 * jj
+                queues[jj % 2].dma_start(T.xs[8 * h + jj], T.x[:, c0:c0 + 32]).then_inc(s, 16)
+        g.wait_ge(sem.la, 128)
+        g.remote_dma_fused(
+            [RemoteDMATransfer(dst_ids=[dst(cid(p, jj, MATE_KS[j // 4]))], dma_engine_mask=1 << jj,
+                               remote_sem=sem.arra, src=T.xs[8 * q + jj], dst=T.ca[j % 4]) for jj in range(8)],
+            local_sem=sem.sent)
+        g.wait_ge(sem.lb, 128)
+        g.remote_dma_fused(
+            [RemoteDMATransfer(dst_ids=[dst(cid(p, jj, FOLD_K))], dma_engine_mask=1 << jj,
+                               remote_sem=sem.arrb, src=T.xs[8 * p + jj], dst=T.cb[j]) for jj in range(8)],
+            local_sem=sem.sent)
+        g.sync.wait_ge(sem.arrr, 16)
+        g.sync.dma_start(T.y[:], T.res[:]).then_inc(sem.stored, 16)
         g.wait_ge(sem.sent, 16)
         g.sync.wait_ge(sem.stored, 16)
-    elif k == MATE_K:
-        g.wait_ge(sem.arra, 8)
+    elif k in MATE_KS:
+        m = MATE_KS.index(k)
+        g.wait_ge(sem.arra, 4)
         g.remote_dma_fused(
             [RemoteDMATransfer(dst_ids=[dst(cid(1 - p, j, FOLD_K))], dma_engine_mask=0xFF, remote_sem=sem.arrb,
-                               srcs=[T.ca[i] for i in range(8)], dsts=[T.cb[8]], alu_op=2)],
+                               srcs=[T.ca[i] for i in range(4)], dsts=[T.cb[8 + m]], alu_op=2)],
             local_sem=sem.sent)
         g.wait_ge(sem.sent, 8)
     elif k == FOLD_K:
-        ga, jb = divmod(j, NB)
-        g.wait_ge(sem.arrb, 16)
+        g.wait_ge(sem.arrb, 8 + 16)
         g.remote_dma_fused(
-            [RemoteDMATransfer(dst_ids=[dst(cid(p, ga * NB + kb, RANK_K)) for kb in range(NB)],
-                               dma_engine_mask=W3_MASK, remote_sem=sem.arrr, srcs=[T.cb[i] for i in range(9)],
-                               dsts=[T.res[jb] for kb in range(NB)], alu_op=2)],
+            [RemoteDMATransfer(dst_ids=[dst(cid(p, j, RANK_K))], dma_engine_mask=0xFFFF, remote_sem=sem.arrr,
+                               srcs=[T.cb[i] for i in range(10)], dsts=[T.res[:]], alu_op=2)],
             local_sem=sem.sent)
-        g.wait_ge(sem.sent, W3_ENG)
+        g.wait_ge(sem.sent, 16)

@@ -28,20 +28,23 @@ def rank_program(g, core, T, topo):
 
     if k == RANK_K:
         q = 1 - p
+        order = [(j + 1 + i) % 8 for i in range(8)]
         queues = [g.sync, g.scalar]
         for h, s in ((q, sem.la), (p, sem.lb)):
-            for jj in range(8):
+            for i, jj in enumerate(order):
                 c0 = 256 * h + 32 * jj
-                queues[jj % 2].dma_start(T.xs[8 * h + jj], T.x[:, c0:c0 + 32]).then_inc(s, 16)
+                queues[i % 2].dma_start(T.xs[8 * h + jj], T.x[:, c0:c0 + 32]).then_inc(s, 16)
         g.wait_ge(sem.la, 128)
         g.remote_dma_fused(
-            [RemoteDMATransfer(dst_ids=[dst(cid(p, jj, MATE_KS[j // 4]))], dma_engine_mask=1 << jj,
-                               remote_sem=sem.arra, src=T.xs[8 * q + jj], dst=T.ca[j % 4]) for jj in range(8)],
+            [RemoteDMATransfer(dst_ids=[dst(cid(p, jj, MATE_KS[j // 4]))], dma_engine_mask=1 << i,
+                               remote_sem=sem.arra, src=T.xs[8 * q + jj], dst=T.ca[j % 4])
+             for i, jj in enumerate(order)],
             local_sem=sem.sent)
         g.wait_ge(sem.lb, 128)
         g.remote_dma_fused(
-            [RemoteDMATransfer(dst_ids=[dst(cid(p, jj, FOLD_K))], dma_engine_mask=1 << jj,
-                               remote_sem=sem.arrb, src=T.xs[8 * p + jj], dst=T.cb[j]) for jj in range(8)],
+            [RemoteDMATransfer(dst_ids=[dst(cid(p, jj, FOLD_K))], dma_engine_mask=1 << i,
+                               remote_sem=sem.arrb, src=T.xs[8 * p + jj], dst=T.cb[j])
+             for i, jj in enumerate(order)],
             local_sem=sem.sent)
         g.sync.wait_ge(sem.arrr, 16)
         g.sync.dma_start(T.y[:], T.res[:]).then_inc(sem.stored, 16)

from concourse.bass import DstId, RemoteDMATransfer

SCRATCH = {
    "xs": ("dram", [16, 128, 32], "bfloat16"),
    "ca": ("dram", [4, 128, 32], "bfloat16"),
    "cb": ("dram", [10, 128, 32], "bfloat16"),
    "res": ("dram", [128, 32], "bfloat16"),
}
SEMAPHORES = ["la", "lb", "sent", "arra", "arrb", "arrr", "stored"]

RANK_K, FOLD_K = 4, 5
MATE_KS = (6, 7)


def rank_program(g, core, T, topo):
    ch = topo.chip(core)
    k = core % 8
    p = ch & 1
    j = ch >> 1
    sem = T.sem

    def cid(pp, jj, kk):
        return (2 * jj + pp) * 8 + kk

    def dst(c):
        a = topo.addr(c)
        return DstId(rid=a[0], pnc=a[1])

    if k == RANK_K:
        q = 1 - p
        order = [(j + 1 + i) % 8 for i in range(8)]
        queues = [g.sync, g.scalar]
        for h, s in ((q, sem.la), (p, sem.lb)):
            for i, jj in enumerate(order):
                c0 = 256 * h + 32 * jj
                queues[i % 2].dma_start(T.xs[8 * h + jj], T.x[:, c0:c0 + 32]).then_inc(s, 16)
        g.wait_ge(sem.la, 128)
        g.remote_dma_fused(
            [RemoteDMATransfer(dst_ids=[dst(cid(p, jj, MATE_KS[j // 4]))], dma_engine_mask=1 << i,
                               remote_sem=sem.arra, src=T.xs[8 * q + jj], dst=T.ca[j % 4])
             for i, jj in enumerate(order)],
            local_sem=sem.sent)
        g.wait_ge(sem.lb, 128)
        g.remote_dma_fused(
            [RemoteDMATransfer(dst_ids=[dst(cid(p, jj, FOLD_K))], dma_engine_mask=1 << i,
                               remote_sem=sem.arrb, src=T.xs[8 * p + jj], dst=T.cb[j])
             for i, jj in enumerate(order)],
            local_sem=sem.sent)
        g.sync.wait_ge(sem.arrr, 16)
        g.sync.dma_start(T.y[:], T.res[:]).then_inc(sem.stored, 16)
        g.wait_ge(sem.sent, 16)
        g.sync.wait_ge(sem.stored, 16)
    elif k in MATE_KS:
        m = MATE_KS.index(k)
        g.wait_ge(sem.arra, 4)
        g.remote_dma_fused(
            [RemoteDMATransfer(dst_ids=[dst(cid(1 - p, j, FOLD_K))], dma_engine_mask=0xFF, remote_sem=sem.arrb,
                               srcs=[T.ca[i] for i in range(4)], dsts=[T.cb[8 + m]], alu_op=2)],
            local_sem=sem.sent)
        g.wait_ge(sem.sent, 8)
    elif k == FOLD_K:
        g.wait_ge(sem.arrb, 8 + 16)
        g.remote_dma_fused(
            [RemoteDMATransfer(dst_ids=[dst(cid(p, j, RANK_K))], dma_engine_mask=0xFFFF, remote_sem=sem.arrr,
                               srcs=[T.cb[i] for i in range(10)], dsts=[T.res[:]], alu_op=2)],
            local_sem=sem.sent)
        g.wait_ge(sem.sent, 16)
